import numpy as np
CORES = [6,14,22,30,38,46,54,62,134,142,150,158,166,174,182,190,262,270,278,286,294,302,310,318,390,398,406,414,422,430,438,446]
N = 32
def setup_inputs(rng):
    return {"x": rng.standard_normal((N, 128, 32), dtype=np.float32)}
def reference(x):
    g = np.ascontiguousarray(x.transpose(1, 2, 0)).reshape(128, 32 * N)
    return {"y": np.broadcast_to(g, (N,) + g.shape)}

@@ -1,0 +1,107 @@
+from concourse.bass import DstId, RemoteDMATransfer
+
+N = 32
+HALF = 16
+QW = 256
+RANK_CORE = 6
+OWNERS = (7, 3)
+OFF_CHIP = 0x00FF
+ON_CHIP = 0xFF00
+
+SCRATCH = {
+    "xs": ("sbuf", [128, N], "float32"),
+    "Y": ("sbuf", [128, N * N], "float32"),
+}
+SEMAPHORES = ["loaded", "sent", "cols", "cable", "plane", "q0", "q1", "q2", "q3", "stored"]
+
+
+def world(h, c, k):
+    return h * 128 + c * 8 + k
+
+
+def column(h, c, d):
+    l = 0 if h in (0, 3) else 1
+    return ((c % 2) * 2 + d) * 8 + l * 4 + c // 2
+
+
+def owner(rack, j):
+    q, i = divmod(j, 8)
+    p, d = divmod(q, 2)
+    l, k = divmod(i, 4)
+    h = ((0, 1), (3, 2))[rack][l]
+    return world(h, 2 * k + p, OWNERS[d])
+
+
+def dst_id(topo, dst, src):
+    rid, pid = topo.addr(dst, src)
+    return DstId(rid=rid, pnc=pid)
+
+
+def rank_core(g, core, T, topo, rank):
+    h, c = topo.host(core), topo.chip(core)
+    rack = topo.rack(h)
+    sem = T.sem
+    g.sync.dma_start(T.xs[:], T.x[:]).then_inc(sem.loaded, 16)
+    g.wait_ge(sem.loaded, 16)
+
+    order = [(column(h, c, 0) + t) % N for t in range(N)]
+    near = [j for j in order if (owner(rack, j) // 8) == core // 8]
+    far = [j for j in order if (owner(rack, j) // 8) != core // 8]
+
+    def one(j, engine):
+        return RemoteDMATransfer(dst_ids=[dst_id(topo, owner(rack, j), core)], dma_engine_mask=1 << engine,
+                                 remote_sem=sem.cols, srcs=[T.xs[:, j:j + 1]],
+                                 dsts=[T.Y[:, j * N + rank:j * N + rank + 1]])
+
+    for b in range(0, len(far), 8):
+        call = [one(j, e) for e, j in enumerate(far[b:b + 8])]
+        if b == 0:
+            call += [one(j, 8 + e) for e, j in enumerate(near)]
+        g.remote_dma_fused(call, local_sem=sem.sent)
+
+    p = c % 2
+    for d, queue in enumerate((g.sync, g.scalar)):
+        for q in (2 * p + d, 2 * (1 - p) + d):
+            queue.wait_ge(sem["q%d" % q], 8)
+            queue.dma_start(T.y[:, q * QW:(q + 1) * QW], T.Y[:, q * QW:(q + 1) * QW]).then_inc(sem.stored, 16)
+    g.wait_ge(sem.sent, N)
+    g.wait_ge(sem.stored, 4 * 16)
+
+
+def owner_core(g, core, T, topo, d):
+    h, c = topo.host(core), topo.chip(core)
+    rack = topo.rack(h)
+    sem = T.sem
+    j = column(h, c, d)
+    q = j // 8
+
+    g.wait_ge(sem.cols, HALF)
+    lo = j * N + rack * HALF
+    rid, pid = topo.addr(world(3 - h, c, core % 8), core)
+    g.remote_dma(T.Y[:, lo:lo + HALF], T.Y[:, lo:lo + HALF], sem.cable, sem.sent, pid, rid, OFF_CHIP)
+
+    g.wait_ge(sem.cable, 8)
+    peers = [owner(rack, q * 8 + i) for i in range(8) if q * 8 + i != j]
+    block = T.Y[:, j * N:(j + 1) * N]
+    g.remote_dma_fused([RemoteDMATransfer(dst_ids=[dst_id(topo, o, core) for o in peers], dma_engine_mask=OFF_CHIP,
+                                          remote_sem=sem.plane, srcs=[block], dsts=[block] * len(peers))],
+                       local_sem=sem.sent)
+
+    g.wait_ge(sem.plane, 7 * 8)
+    quarter = T.Y[:, q * QW:(q + 1) * QW]
+    arrived = sem["q%d" % q]
+    g.remote_dma_fused([
+        RemoteDMATransfer(dst_ids=[dst_id(topo, world(h, c ^ 1, RANK_CORE), core)], dma_engine_mask=OFF_CHIP,
+                          remote_sem=arrived, srcs=[quarter], dsts=[quarter]),
+        RemoteDMATransfer(dst_ids=[dst_id(topo, world(h, c, RANK_CORE), core)], dma_engine_mask=ON_CHIP,
+                          remote_sem=arrived, srcs=[quarter], dsts=[quarter]),
+    ], local_sem=sem.sent)
+    g.wait_ge(sem.sent, 8 + 8 + 16)
+
+
+def rank_program(g, core, T, topo):
+    rank = T.rank_of(core)
+    if rank is not None:
+        rank_core(g, core, T, topo, rank)
+    elif topo.chip(core) < 8 and core % 8 in OWNERS:
+        owner_core(g, core, T, topo, OWNERS.index(core % 8))

@@ -2,34 +2,40 @@ from concourse.bass import DstId, RemoteDMATransfer
 
 N = 32
 HALF = 16
-QW = 256
 RANK_CORE = 6
 OWNERS = (7, 3)
 OFF_CHIP = 0x00FF
-ON_CHIP = 0xFF00
 
 SCRATCH = {
-    "xs": ("sbuf", [128, N], "float32"),
-    "Y": ("sbuf", [128, N * N], "float32"),
+    "xd": ("dram", [N, 128, 1], "float32"),
+    "blk": ("sbuf", [128, N], "float32"),
+    "Yd": ("dram", [N, 128, N], "float32"),
 }
-SEMAPHORES = ["loaded", "sent", "cols", "cable", "plane", "q0", "q1", "q2", "q3", "stored"]
+SEMAPHORES = ["loaded", "sent", "share", "cols", "cable", "packed", "plane", "q0", "q1", "q2", "q3", "stored"]
 
 
 def world(h, c, k):
     return h * 128 + c * 8 + k
 
 
-def column(h, c, d):
+def slot_of(h, c, d):
     l = 0 if h in (0, 3) else 1
     return ((c % 2) * 2 + d) * 8 + l * 4 + c // 2
 
 
-def owner(rack, j):
-    q, i = divmod(j, 8)
+def owner(rack, s):
+    q, i = divmod(s, 8)
     p, d = divmod(q, 2)
     l, k = divmod(i, 4)
     h = ((0, 1), (3, 2))[rack][l]
     return world(h, 2 * k + p, OWNERS[d])
+
+
+def scattered_by(c, k):
+    d = 0 if k >= 4 else 1
+    p = (c % 2) ^ (1 if k % 4 >= 2 else 0)
+    first = (2 * p + d) * 8 + (k % 2) * 4
+    return list(range(first, first + 4))
 
 
 def dst_id(topo, dst, src):
@@ -37,71 +43,75 @@ def dst_id(topo, dst, src):
     return DstId(rid=rid, pnc=pid)
 
 
-def rank_core(g, core, T, topo, rank):
+def scatter(g, core, T, topo):
+    h, c, k = topo.host(core), topo.chip(core), core % 8
+    r = T.rank_of(world(h, c, RANK_CORE))
+    g.remote_dma_fused([
+        RemoteDMATransfer(dst_ids=[dst_id(topo, owner(topo.rack(h), s), core)], dma_engine_mask=3 << (2 * e),
+                          remote_sem=T.sem.cols, srcs=[T.xd[s]], dsts=[T.blk[:, r:r + 1]])
+        for e, s in enumerate(scattered_by(c, k))], local_sem=T.sem.sent)
+
+
+def rank_core(g, core, T, topo):
     h, c = topo.host(core), topo.chip(core)
-    rack = topo.rack(h)
     sem = T.sem
-    g.sync.dma_start(T.xs[:], T.x[:]).then_inc(sem.loaded, 16)
+    g.sync.dma_start(T.xd[:], T.x[:]).then_inc(sem.loaded, 16)
     g.wait_ge(sem.loaded, 16)
 
-    order = [(column(h, c, 0) + t) % N for t in range(N)]
-    near = [j for j in order if (owner(rack, j) // 8) == core // 8]
-    far = [j for j in order if (owner(rack, j) // 8) != core // 8]
-
-    def one(j, engine):
-        return RemoteDMATransfer(dst_ids=[dst_id(topo, owner(rack, j), core)], dma_engine_mask=1 << engine,
-                                 remote_sem=sem.cols, srcs=[T.xs[:, j:j + 1]],
-                                 dsts=[T.Y[:, j * N + rank:j * N + rank + 1]])
-
-    for b in range(0, len(far), 8):
-        call = [one(j, e) for e, j in enumerate(far[b:b + 8])]
-        if b == 0:
-            call += [one(j, 8 + e) for e, j in enumerate(near)]
-        g.remote_dma_fused(call, local_sem=sem.sent)
+    shares = [(k, s) for k in range(8) if k != RANK_CORE for s in scattered_by(c, k)]
+    for b in range(0, len(shares), 16):
+        g.remote_dma_fused([
+            RemoteDMATransfer(dst_ids=[dst_id(topo, world(h, c, k), core)], dma_engine_mask=1 << e,
+                              remote_sem=sem.share, srcs=[T.xd[s]], dsts=[T.xd[s]])
+            for e, (k, s) in enumerate(shares[b:b + 16])], local_sem=sem.sent)
+    scatter(g, core, T, topo)
 
     p = c % 2
     for d, queue in enumerate((g.sync, g.scalar)):
         for q in (2 * p + d, 2 * (1 - p) + d):
             queue.wait_ge(sem["q%d" % q], 8)
-            queue.dma_start(T.y[:, q * QW:(q + 1) * QW], T.Y[:, q * QW:(q + 1) * QW]).then_inc(sem.stored, 16)
-    g.wait_ge(sem.sent, N)
+            queue.dma_start(T.y[32 * q:32 * q + 32, :], T.Yd[8 * q:8 * q + 8]).then_inc(sem.stored, 16)
+    g.wait_ge(sem.sent, len(shares) + 8)
     g.wait_ge(sem.stored, 4 * 16)
 
 
-def owner_core(g, core, T, topo, d):
-    h, c = topo.host(core), topo.chip(core)
+def helper_core(g, core, T, topo):
+    h, c, k = topo.host(core), topo.chip(core), core % 8
     rack = topo.rack(h)
     sem = T.sem
-    j = column(h, c, d)
-    q = j // 8
+    g.wait_ge(sem.share, 4)
+    scatter(g, core, T, topo)
+    if k not in OWNERS:
+        g.wait_ge(sem.sent, 8)
+        return
+    s = slot_of(h, c, OWNERS.index(k))
+    q = s // 8
 
-    g.wait_ge(sem.cols, HALF)
-    lo = j * N + rack * HALF
-    rid, pid = topo.addr(world(3 - h, c, core % 8), core)
-    g.remote_dma(T.Y[:, lo:lo + HALF], T.Y[:, lo:lo + HALF], sem.cable, sem.sent, pid, rid, OFF_CHIP)
+    g.wait_ge(sem.cols, 2 * HALF)
+    half = T.blk[:, rack * HALF:(rack + 1) * HALF]
+    rid, pid = topo.addr(world(3 - h, c, k), core)
+    g.remote_dma(half, half, sem.cable, sem.sent, pid, rid, OFF_CHIP)
 
-    g.wait_ge(sem.cable, 8)
-    peers = [owner(rack, q * 8 + i) for i in range(8) if q * 8 + i != j]
-    block = T.Y[:, j * N:(j + 1) * N]
+    g.sync.wait_ge(sem.cols, 2 * HALF)
+    g.sync.wait_ge(sem.cable, 8)
+    g.sync.dma_start(T.Yd[s], T.blk[:]).then_inc(sem.packed, 16)
+
+    g.wait_ge(sem.packed, 16)
+    peers = [owner(rack, t) for t in range(8 * q, 8 * q + 8) if t != s]
     g.remote_dma_fused([RemoteDMATransfer(dst_ids=[dst_id(topo, o, core) for o in peers], dma_engine_mask=OFF_CHIP,
-                                          remote_sem=sem.plane, srcs=[block], dsts=[block] * len(peers))],
+                                          remote_sem=sem.plane, srcs=[T.Yd[s]], dsts=[T.Yd[s]] * len(peers))],
                        local_sem=sem.sent)
 
     g.wait_ge(sem.plane, 7 * 8)
-    quarter = T.Y[:, q * QW:(q + 1) * QW]
-    arrived = sem["q%d" % q]
     g.remote_dma_fused([
-        RemoteDMATransfer(dst_ids=[dst_id(topo, world(h, c ^ 1, RANK_CORE), core)], dma_engine_mask=OFF_CHIP,
-                          remote_sem=arrived, srcs=[quarter], dsts=[quarter]),
-        RemoteDMATransfer(dst_ids=[dst_id(topo, world(h, c, RANK_CORE), core)], dma_engine_mask=ON_CHIP,
-                          remote_sem=arrived, srcs=[quarter], dsts=[quarter]),
-    ], local_sem=sem.sent)
-    g.wait_ge(sem.sent, 8 + 8 + 16)
+        RemoteDMATransfer(dst_ids=[dst_id(topo, world(h, cc, RANK_CORE), core)], dma_engine_mask=1 << (base + i),
+                          remote_sem=sem["q%d" % q], srcs=[T.Yd[8 * q + i]], dsts=[T.Yd[8 * q + i]])
+        for cc, base in ((c ^ 1, 0), (c, 8)) for i in range(8)], local_sem=sem.sent)
+    g.wait_ge(sem.sent, 8 + 8 + 8 + 16)
 
 
 def rank_program(g, core, T, topo):
-    rank = T.rank_of(core)
-    if rank is not None:
-        rank_core(g, core, T, topo, rank)
-    elif topo.chip(core) < 8 and core % 8 in OWNERS:
-        owner_core(g, core, T, topo, OWNERS.index(core % 8))
+    if T.rank_of(core) is not None:
+        rank_core(g, core, T, topo)
+    elif topo.chip(core) < 8:
+        helper_core(g, core, T, topo)

from concourse.bass import DstId, RemoteDMATransfer

N = 32
HALF = 16
RANK_CORE = 6
OWNERS = (7, 3)
OFF_CHIP = 0x00FF

SCRATCH = {
    "xd": ("dram", [N, 128, 1], "float32"),
    "blk": ("sbuf", [128, N], "float32"),
    "Yd": ("dram", [N, 128, N], "float32"),
}
SEMAPHORES = ["loaded", "sent", "share", "cols", "cable", "packed", "plane", "q0", "q1", "q2", "q3", "stored"]


def world(h, c, k):
    return h * 128 + c * 8 + k


def slot_of(h, c, d):
    l = 0 if h in (0, 3) else 1
    return ((c % 2) * 2 + d) * 8 + l * 4 + c // 2


def owner(rack, s):
    q, i = divmod(s, 8)
    p, d = divmod(q, 2)
    l, k = divmod(i, 4)
    h = ((0, 1), (3, 2))[rack][l]
    return world(h, 2 * k + p, OWNERS[d])


def scattered_by(c, k):
    d = 0 if k >= 4 else 1
    p = (c % 2) ^ (1 if k % 4 >= 2 else 0)
    first = (2 * p + d) * 8 + (k % 2) * 4
    return list(range(first, first + 4))


def dst_id(topo, dst, src):
    rid, pid = topo.addr(dst, src)
    return DstId(rid=rid, pnc=pid)


def scatter(g, core, T, topo):
    h, c, k = topo.host(core), topo.chip(core), core % 8
    r = T.rank_of(world(h, c, RANK_CORE))
    g.remote_dma_fused([
        RemoteDMATransfer(dst_ids=[dst_id(topo, owner(topo.rack(h), s), core)], dma_engine_mask=3 << (2 * e),
                          remote_sem=T.sem.cols, srcs=[T.xd[s]], dsts=[T.blk[:, r:r + 1]])
        for e, s in enumerate(scattered_by(c, k))], local_sem=T.sem.sent)


def rank_core(g, core, T, topo):
    h, c = topo.host(core), topo.chip(core)
    sem = T.sem
    g.sync.dma_start(T.xd[:], T.x[:]).then_inc(sem.loaded, 16)
    g.wait_ge(sem.loaded, 16)

    shares = [(k, s) for k in range(8) if k != RANK_CORE for s in scattered_by(c, k)]
    for b in range(0, len(shares), 16):
        g.remote_dma_fused([
            RemoteDMATransfer(dst_ids=[dst_id(topo, world(h, c, k), core)], dma_engine_mask=1 << e,
                              remote_sem=sem.share, srcs=[T.xd[s]], dsts=[T.xd[s]])
            for e, (k, s) in enumerate(shares[b:b + 16])], local_sem=sem.sent)
    scatter(g, core, T, topo)

    p = c % 2
    for d, queue in enumerate((g.sync, g.scalar)):
        for q in (2 * p + d, 2 * (1 - p) + d):
            queue.wait_ge(sem["q%d" % q], 8)
            queue.dma_start(T.y[32 * q:32 * q + 32, :], T.Yd[8 * q:8 * q + 8]).then_inc(sem.stored, 16)
    g.wait_ge(sem.sent, len(shares) + 8)
    g.wait_ge(sem.stored, 4 * 16)


def helper_core(g, core, T, topo):
    h, c, k = topo.host(core), topo.chip(core), core % 8
    rack = topo.rack(h)
    sem = T.sem
    g.wait_ge(sem.share, 4)
    scatter(g, core, T, topo)
    if k not in OWNERS:
        g.wait_ge(sem.sent, 8)
        return
    s = slot_of(h, c, OWNERS.index(k))
    q = s // 8

    g.wait_ge(sem.cols, 2 * HALF)
    half = T.blk[:, rack * HALF:(rack + 1) * HALF]
    rid, pid = topo.addr(world(3 - h, c, k), core)
    g.remote_dma(half, half, sem.cable, sem.sent, pid, rid, OFF_CHIP)

    g.sync.wait_ge(sem.cols, 2 * HALF)
    g.sync.wait_ge(sem.cable, 8)
    g.sync.dma_start(T.Yd[s], T.blk[:]).then_inc(sem.packed, 16)

    g.wait_ge(sem.packed, 16)
    peers = [owner(rack, t) for t in range(8 * q, 8 * q + 8) if t != s]
    g.remote_dma_fused([RemoteDMATransfer(dst_ids=[dst_id(topo, o, core) for o in peers], dma_engine_mask=OFF_CHIP,
                                          remote_sem=sem.plane, srcs=[T.Yd[s]], dsts=[T.Yd[s]] * len(peers))],
                       local_sem=sem.sent)

    g.wait_ge(sem.plane, 7 * 8)
    g.remote_dma_fused([
        RemoteDMATransfer(dst_ids=[dst_id(topo, world(h, cc, RANK_CORE), core)], dma_engine_mask=1 << (base + i),
                          remote_sem=sem["q%d" % q], srcs=[T.Yd[8 * q + i]], dsts=[T.Yd[8 * q + i]])
        for cc, base in ((c ^ 1, 0), (c, 8)) for i in range(8)], local_sem=sem.sent)
    g.wait_ge(sem.sent, 8 + 8 + 8 + 16)


def rank_program(g, core, T, topo):
    if T.rank_of(core) is not None:
        rank_core(g, core, T, topo)
    elif topo.chip(core) < 8:
        helper_core(g, core, T, topo)
